import numpy as np, ml_dtypes
CORES = [3,7,11,15,131,135,139,143]
N = 8
import mx_ref
NC, ROOT = 256, 1
A = np.float32(0.0125)
BF = ml_dtypes.bfloat16
def cut(t, i, w=512):
    return t[:, w * i:w * i + w]
def tile(rs):
    return np.stack(rs, axis=2).reshape(128, -1).astype(BF)
def pk(c, s, i=0):
    return (np.ascontiguousarray(c[:, 512 * i:512 * i + 512]), mx_ref.live(s[:, 128 * i:128 * i + 128]))
def raw(rng):
    def f(*shape):
        return mx_ref.flush((rng.standard_normal(shape, dtype=np.float32) * np.exp2(rng.integers(-2, 3, shape[:-1] + (1,)))).astype(BF))
    return {"q": f(N, 128, 4 * NC), "k": f(N, 128, 4 * 512), "v": f(N, 128, 512)}
def raw_blocks(rng):
    d = raw(rng)
    for k in ("v",): d[k] = mx_ref.spread(d[k], rng, 4)
    for k in ("q", "k"): d[k] = mx_ref.spread(d[k], rng, 1)
    return d
def raw_wide(rng):
    d = raw(rng)
    for k in ("v",): d[k] = mx_ref.flush((d[k].astype(np.float32) * np.exp2(rng.integers(-8, 9, (N, 1, 1))).astype(np.float32)).astype(BF))
    return d
def raw_sharp(rng):
    d = raw(rng); v = d["q"].astype(np.float32).reshape(N, 128, -1, 4)
    d["q"] = mx_ref.flush((v * np.exp2(rng.integers(-2, 4, (N, 1, v.shape[2], 1))).astype(np.float32)).reshape(d["q"].shape).astype(BF))
    return d
def raw_offset(rng):
    d = raw(rng); v = d["k"].astype(np.float32).reshape(N, 128, -1, 4)
    d["k"] = mx_ref.flush((v + 12 * rng.standard_normal((1, 128, 1, 4), dtype=np.float32)).reshape(d["k"].shape).astype(BF))
    return d
def pack(d, rng):
    o = {"q": d["q"]}
    for m in ("k", "v"):
        t = d[m]; c = np.zeros(t.shape, np.uint8); s = np.zeros((N, 128, t.shape[2] // 4), np.uint8)
        for r in range(N):
            for i in range(t.shape[2] // 512):
                a, b = mx_ref.quantize(cut(t[r], i)); c[r][:, 512 * i:512 * i + 512] = a; s[r][:, 128 * i:128 * i + 128] = mx_ref.plane(b, rng)
        o[m + "c"], o[m + "s"] = c, s
    return o
def setup_inputs(rng):
    return pack(raw(rng), rng)
def setup_inputs_blocks(rng):
    return pack(raw_blocks(rng), rng)
def setup_inputs_offset(rng):
    return pack(raw_offset(rng), rng)
def setup_inputs_sharp(rng):
    return pack(raw_sharp(rng), rng)
def setup_inputs_wide(rng):
    return pack(raw_wide(rng), rng)
def reference(q, kc, ks, vc, vs, own=None):
    ONE = mx_ref.quantize(np.ones((128, 512), BF)); Q = mx_ref.quantize(q[ROOT])
    S = [[mx_ref.matmul(pk(kc[j], ks[j], b), Q) * A for b in range(4)] for j in range(N)]
    lo = np.stack([np.max(s, axis=(0, 1))[None] for s in S]); hi = np.broadcast_to(lo.max(axis=0) + 8, lo.shape).copy()
    c = lo if own is None else own["c"]
    p = np.stack([tile([np.exp(np.maximum(s - c[j], -20).astype(np.float64)).astype(np.float32) for s in S[j]]) for j in range(N)])
    use = p if own is None else own["p"]
    e = np.exp((c - c.max(axis=0)).astype(np.float64))[:, 0]; wlo = np.zeros((N, N, NC), np.float32); whi = np.ones((N, N, NC), np.float32); wlo[ROOT] = e * (1 - 4e-5); whi[ROOT] = e * (1 + 4e-5)
    w = np.zeros((N, N, NC), np.float32); w[ROOT] = e
    if own is not None: w = own["w"]
    num = den = 0
    for j in range(N):
        P = mx_ref.quantize(use[j])
        num = num + w[ROOT][j].astype(np.float64) * mx_ref.matmul(pk(vc[j], vs[j]), P); den = den + w[ROOT][j].astype(np.float64) * mx_ref.matmul(ONE, P)
    o = np.full((N, 128, NC), np.nan, np.float32); o[ROOT] = (num / den).astype(np.float32)
    return {"c": c, "c__lo": lo, "c__hi": hi, "p": p, "w": w, "w__lo": wlo, "w__hi": whi, "o": o}

@@ -1,0 +1,364 @@
+import numpy as np
+from concourse.mybir import dt, AluOpType, AxisListType, ActivationFunctionType
+
+N = 8
+MODE = "direct"
+NCH = 1
+SL = 132
+F32, BF, CODE, U8 = "float32", "bfloat16", "float8_e4m3fn_x4", "uint8"
+
+SCRATCH = {
+    "qt": ("sbuf", [128, 1024], BF), "qc": ("sbuf", [128, 256], CODE), "qs": ("sbuf", [128, 256], U8),
+    "kcb": ("sbuf", [128, 512], CODE), "ksb": ("sbuf", [128, 512], U8),
+    "vo": ("sbuf", [128, 256], CODE), "vos": ("sbuf", [128, 256], U8),
+    "onet": ("sbuf", [128, 512], BF), "atile": ("sbuf", [128, 128], F32),
+    "n20": ("sbuf", [128, 1], F32), "e20": ("sbuf", [128, 1], BF),
+    "mT": ("sbuf", [128, 2], F32), "cT": ("sbuf", [128, 2], F32),
+    "E": ("sbuf", [128, 256], F32), "C": ("sbuf", [128, 256], F32),
+    "SA": ("sbuf", [128, 1024], F32), "X": ("sbuf", [128, 1024], F32),
+    "P": ("sbuf", [128, 1024], BF), "pc": ("sbuf", [128, 256], CODE), "psc": ("sbuf", [128, 256], U8),
+    "msg": ("sbuf", [128, 2 * SL], F32), "zw": ("sbuf", [128, 256], F32),
+    "cland": ("sbuf", [128, 4 * N], F32), "negM": ("sbuf", [128, 2], F32),
+    "wx": ("sbuf", [128, 64], F32), "wxt": ("sbuf", [128, 64], F32),
+    "aland": ("sbuf", [128, 2 * N * SL], F32), "tmp": ("sbuf", [128, 2 * N * SL], F32),
+    "acc": ("sbuf", [128, 2 * SL], F32), "rdn": ("sbuf", [128, 2], F32),
+    "Z": ("sbuf", [128, 256], F32), "Zt": ("sbuf", [128, 256], F32), "O": ("sbuf", [128, 256], F32),
+    "ps": ("psum", [128, 4096], F32),
+}
+
+SEMAPHORES = (
+    ["ldq", "ldk", "m_one", "m_at", "m_n20", "m_wx", "m_zw", "qone", "e20s", "qq", "tr", "ct", "sent",
+     "outc", "outp", "outw", "outo", "qarr0", "qarr1", "carr", "ng", "wxs", "wt"]
+    + ["%s%d" % (n, h) for n in ("st", "rd", "xp", "ex", "cl", "qp", "al", "ev", "tmo", "ac", "rc", "z", "zt", "cpv", "cps")
+       for h in range(2)]
+    + ["%s%d" % (n, b) for n in ("sb", "sa") for b in range(4)]
+    + ["%s_%d%s" % (n, h, s) for n in ("s1", "s2") for h in range(2) for s in ("l", "h")]
+    + ["x%d%d" % (h, b) for h in range(2) for b in range(4)]
+    + ["%s%d_%d" % (n, j, h) for n in ("ar", "tm") for j in range(N) for h in range(2)]
+)
+
+
+def rank_program(g, core, T, topo):
+    rank = T.rank_of(core)
+    if rank is None:
+        return
+    sem = T.sem
+    root = T.root
+    rootc = T.cores[root]
+    is_root = rank == root
+    V, S, PE, SY = g.vector, g.scalar, g.tensor, g.sync
+    u8 = dt.uint8
+    ALU, ACT, AX = AluOpType, ActivationFunctionType, AxisListType
+    A = float(np.float32(0.0125))
+
+    tot, seen = {}, {}
+
+    def inc(ins, name, n=1):
+        ins.then_inc(sem[name], n)
+        tot[name] = tot.get(name, 0) + n
+
+    def wait(q, name, n=None):
+        n = tot[name] if n is None else n
+        q.wait_ge(sem[name], n)
+        seen[name] = max(seen.get(name, 0), n)
+
+    def engines(m):
+        return bin(m).count("1")
+
+    def same_chip(a, b):
+        return topo.host(a) == topo.host(b) and topo.chip(a) == topo.chip(b)
+
+    def far(a, b):
+        if same_chip(a, b):
+            return 0
+        return 1 if (topo.mates(a, b) or topo.same_plane(a, b)) else 2
+
+    others = [r for r in range(N) if r != root]
+    near = [r for r in others if same_chip(T.cores[r], rootc)]
+    off = sorted([r for r in others if r not in near], key=lambda r: -far(rootc, T.cores[r]))
+    leave = 0
+    for r in off:
+        leave |= topo.mask(rootc, T.cores[r])
+
+    def qmask(a, r):
+        m = topo.mask(T.cores[a], T.cores[r])
+        if same_chip(T.cores[a], T.cores[r]) and (m & ~leave):
+            m &= ~leave
+        return m
+    mine = [r for r in off if topo.die(T.cores[r]) == topo.die(rootc)]
+    his = [r for r in off if r not in mine]
+    if MODE == "direct":
+        plan = {root: off[:1] + near + off[1:]}
+        proc = near + off
+    elif MODE == "two":
+        plan = {root: near[:1] + mine, near[0]: his}
+        proc = near + [r for pair in zip(mine, his) for r in pair]
+    else:
+        plan = {root: near[:1] + [r for r in mine if far(rootc, T.cores[r]) == 1]}
+        for r in mine:
+            if far(rootc, T.cores[r]) == 2:
+                up = [x for x in mine if far(rootc, T.cores[x]) == 1 and topo.same_plane(T.cores[x], T.cores[r])][0]
+                plan[up] = plan.get(up, []) + [r]
+        for r in his:
+            if far(rootc, T.cores[r]) == 2:
+                plan[near[0]] = plan.get(near[0], []) + [r]
+            else:
+                up = [x for x in mine if same_chip(T.cores[x], T.cores[r])][0]
+                plan[up] = plan.get(up, []) + [r]
+        proc = near + [r for r in off if far(rootc, T.cores[r]) == 1] + [r for r in off if far(rootc, T.cores[r]) == 2]
+    parent = {}
+    for a in plan:
+        for r in plan[a]:
+            parent[r] = a
+    CW = 256 // NCH
+
+    def vcopy(out, in_):
+        return V.tensor_copy(out, in_)
+
+    def scopy(out, in_):
+        return S.activation(out, in_, ACT.Identity)
+
+    if is_root:
+        inc(SY.dma_start(T.qt[:], T.q[:]), "ldq", 16)
+        wait(SY, "ldq")
+    inc(SY.dma_start(T.kcb[:].bitcast(u8), T.kc[:]), "ldk", 16)
+    inc(SY.dma_start(T.ksb[:], T.ks[:]), "ldk", 16)
+    inc(SY.dma_start(T.vo[:, 0:128].bitcast(u8), T.vc[:]), "ldk", 16)
+    inc(SY.dma_start(T.vos[:, 0:128], T.vs[:]), "ldk", 16)
+
+    inc(V.memset(T.onet[:], 1.0), "m_one")
+    inc(V.memset(T.atile[:], A), "m_at")
+    inc(V.memset(T.n20[:], -20.0), "m_n20")
+    if is_root:
+        inc(V.memset(T.wx[:], 0.0), "m_wx")
+    else:
+        inc(V.memset(T.zw[0:8, :], 0.0), "m_zw")
+        wait(SY, "m_zw")
+        inc(SY.dma_start(T.w[:], T.zw[0:8, :]), "outw", 16)
+    wait(V, "m_one")
+    inc(V.quantize_mx(T.vo[:, 128:256], T.vos[:, 128:256], T.onet[:]), "qone")
+    wait(S, "m_n20")
+    inc(S.activation(T.e20[:], T.n20[:], ACT.Exp), "e20s")
+
+    nsent = 0
+    if is_root:
+        wait(V, "ldq")
+        inc(V.quantize_mx(T.qc[:], T.qs[:], T.qt[:]), "qq")
+        wait(g, "qq")
+    nq = 0 if is_root else 2 * engines(qmask(parent[rank], rank))
+    got = [is_root] * NCH
+    for r in plan.get(rank, []):
+        qrid, qpid = topo.addr(T.cores[r], core)
+        m = qmask(rank, r)
+        for k in range(NCH):
+            if not got[k]:
+                g.wait_ge(sem["qarr%d" % k], nq)
+                got[k] = True
+            cs = slice(CW * k, CW * k + CW)
+            g.remote_dma(out_ap=T.qc[:, cs].bitcast(u8), in_ap=T.qc[:, cs].bitcast(u8), remote_sem=sem["qarr%d" % k],
+                         local_sem=sem.sent, pid=qpid, routing_id=qrid, dma_engine_mask=m)
+            g.remote_dma(out_ap=T.qs[:, cs], in_ap=T.qs[:, cs], remote_sem=sem["qarr%d" % k], local_sem=sem.sent,
+                         pid=qpid, routing_id=qrid, dma_engine_mask=m)
+            nsent += 2 * engines(m)
+
+    wait(PE, "ldk")
+    if is_root:
+        wait(PE, "qq")
+    for h in range(2):
+        if not is_root and (h == 0 or NCH == 2):
+            PE.wait_ge(sem["qarr%d" % (h if NCH == 2 else 0)], nq)
+        inc(PE.matmul_mx(T.ps[:, 512 * h:512 * h + 512], T.qc[:, 128 * h:128 * h + 128], T.qs[:, 128 * h:128 * h + 128],
+                         T.kcb[:], T.ksb[:], True, True), "st%d" % h)
+    for b in range(4):
+        inc(PE.matmul_mx(T.ps[:, 1024 + 512 * b:1024 + 512 * b + 256], T.kcb[:, 128 * b:128 * b + 128],
+                         T.ksb[:, 128 * b:128 * b + 128], T.qc[:], T.qs[:], True, True), "sb%d" % b)
+
+    def scale(b):
+        wait(S, "sb%d" % b)
+        inc(S.activation(T.SA[:, 256 * b:256 * b + 256], T.ps[:, 1024 + 512 * b:1024 + 512 * b + 256], ACT.Identity, scale=A),
+            "sa%d" % b)
+
+    wait(V, "st0")
+    inc(V.tensor_reduce(T.mT[:, 0:1], T.ps[:, 0:512], AX.X, ALU.max), "rd0")
+    wait(S, "rd0")
+    wait(S, "m_at")
+    inc(S.activation(T.E[:, 0:128], T.atile[:], ACT.Identity, scale=T.mT[:, 0:1]), "xp0")
+    wait(V, "st1")
+    inc(V.tensor_reduce(T.mT[:, 1:2], T.ps[:, 512:1024], AX.X, ALU.max), "rd1")
+    wait(V, "rd1")
+    wait(V, "m_at")
+    inc(V.tensor_scalar(T.E[:, 128:256], T.atile[:], T.mT[:, 1:2], None, ALU.mult), "xp1")
+    scale(0)
+    scale(1)
+    wait(V, "xp0")
+    wait(V, "xp1")
+    inc(V.transpose(T.C[:], T.E[:]), "tr")
+
+    def spread(q, copy, h, s):
+        lo = 0 if s == "l" else 2
+        wait(q, "tr")
+        for a in (lo, lo + 1):
+            o = lo + 1 if a == lo else lo
+            c0 = 128 * h + 32 * a
+            inc(copy(T.C[32 * o:32 * o + 32, c0:c0 + 32], T.C[32 * a:32 * a + 32, c0:c0 + 32]), "s1_%d%s" % (h, s))
+        wait(q, "s1_%d%s" % (h, s))
+        c0 = 128 * h + 32 * lo
+        src, dst = (0, 64) if s == "l" else (64, 0)
+        inc(copy(T.C[dst:dst + 64, c0:c0 + 64], T.C[src:src + 64, c0:c0 + 64]), "s2_%d%s" % (h, s))
+
+    spread(V, vcopy, 0, "l")
+    spread(S, scopy, 0, "h")
+    scale(2)
+    spread(S, scopy, 1, "l")
+    spread(S, scopy, 1, "h")
+    scale(3)
+    wait(S, "rd1")
+    cdst = T.cland[:, 4 * rank:4 * rank + 2] if is_root else T.cT[:]
+    inc(S.activation(cdst, T.mT[:], ACT.Identity, scale=A), "ct")
+    for h in range(2):
+        for s in ("l", "h"):
+            wait(SY, "s2_%d%s" % (h, s))
+    inc(SY.dma_start(T.c[:], T.C[0:1, :]), "outc", 16)
+
+    rid, pid = (None, None) if is_root else topo.addr(rootc, core)
+    mk = 0 if is_root else topo.mask(core, rootc)
+    if not is_root:
+        wait(g, "ct")
+        g.remote_dma(out_ap=T.cland[:, 4 * rank:4 * rank + 2], in_ap=T.cT[:], remote_sem=sem.carr, local_sem=sem.sent,
+                     pid=pid, routing_id=rid, dma_engine_mask=mk)
+        nsent += engines(mk)
+
+    def sub_exp(h, b):
+        c0 = 256 * b + 128 * h
+        wait(V, "sa%d" % b)
+        wait(V, "s2_%dl" % h)
+        wait(V, "s2_%dh" % h)
+        inc(V.tensor_tensor(T.X[:, c0:c0 + 128], T.SA[:, c0:c0 + 128], T.C[:, 128 * h:128 * h + 128], ALU.subtract),
+            "x%d%d" % (h, b))
+        wait(S, "x%d%d" % (h, b))
+        inc(S.activation(T.P[:, 512 * h + b:512 * h + 512:4], T.X[:, c0:c0 + 128], ACT.Exp), "ex%d" % h)
+
+    def finish(h):
+        wait(V, "ex%d" % h)
+        wait(V, "e20s")
+        inc(V.tensor_scalar(T.P[:, 512 * h:512 * h + 512], T.P[:, 512 * h:512 * h + 512], T.e20[:, 0:1], None, ALU.max),
+            "cl%d" % h)
+        wait(V, "cl%d" % h)
+        inc(V.quantize_mx(T.pc[:, 128 * h:128 * h + 128], T.psc[:, 128 * h:128 * h + 128], T.P[:, 512 * h:512 * h + 512]),
+            "qp%d" % h)
+        wait(SY, "cl%d" % h)
+        inc(SY.dma_start(T.p[:, 512 * h:512 * h + 512], T.P[:, 512 * h:512 * h + 512]), "outp", 16)
+        wait(PE, "qp%d" % h)
+        wait(PE, "qone")
+        inc(PE.matmul_mx(T.ps[:, 3072 + 512 * h:3072 + 512 * h + 256], T.pc[:, 128 * h:128 * h + 128],
+                         T.psc[:, 128 * h:128 * h + 128], T.vo[:], T.vos[:], True, True), "al%d" % h)
+
+    def ship(h):
+        wait(S, "al%d" % h)
+        inc(scopy(T.msg[:, SL * h:SL * h + 129], T.ps[:, 3072 + 512 * h:3072 + 512 * h + 129]), "ev%d" % h)
+        wait(g, "ev%d" % h)
+        s0 = SL * (2 * rank + h)
+        g.remote_dma(out_ap=T.aland[:, s0:s0 + 129], in_ap=T.msg[:, SL * h:SL * h + 129], remote_sem=sem["ar%d_%d" % (rank, h)],
+                     local_sem=sem.sent, pid=pid, routing_id=rid, dma_engine_mask=mk)
+
+    for h, b in ((0, 0), (0, 1), (0, 2), (1, 0), (0, 3), (1, 1)):
+        sub_exp(h, b)
+    finish(0)
+    sub_exp(1, 2)
+    if not is_root:
+        ship(0)
+    sub_exp(1, 3)
+    finish(1)
+    if not is_root:
+        ship(1)
+        nsent += 2 * engines(mk)
+
+    if is_root:
+        ncarr = 0
+        for r in others:
+            ncarr += engines(topo.mask(T.cores[r], rootc))
+        V.wait_ge(sem.carr, ncarr)
+        wait(V, "ct")
+        for h in range(2):
+            inc(V.tensor_reduce(T.negM[:, h:h + 1], T.cland[:, h:4 * N:4], AX.X, ALU.max, negate=True), "ng")
+        wait(S, "ng")
+        wait(S, "m_wx")
+        for h in range(2):
+            inc(S.activation(T.wx[:, 32 * h:32 * h + N], T.cland[:, h:4 * N:4], ACT.Exp, bias=T.negM[:, h:h + 1]), "wxs")
+        wait(V, "wxs")
+        inc(V.transpose(T.wxt[:], T.wx[:]), "wt")
+        wait(SY, "wt")
+        for h in range(2):
+            for a in range(4):
+                c0 = 128 * h + 32 * a
+                inc(SY.dma_start(T.w[:, c0:c0 + 32], T.wxt[32 * a:32 * a + N, 32 * h:32 * h + 32]), "outw", 16)
+        wait(S, "wxs")
+        for h in range(2):
+            s0 = SL * (2 * rank + h)
+            wait(S, "al%d" % h)
+            inc(S.activation(T.tmp[:, s0:s0 + 129], T.ps[:, 3072 + 512 * h:3072 + 512 * h + 129], ACT.Identity,
+                             scale=T.wx[:, 32 * h + rank:32 * h + rank + 1]), "tmo%d" % h)
+
+        def weigh(j, h):
+            s0 = SL * (2 * j + h)
+            S.wait_ge(sem["ar%d_%d" % (j, h)], engines(topo.mask(T.cores[j], rootc)))
+            inc(S.activation(T.tmp[:, s0:s0 + 129], T.aland[:, s0:s0 + 129], ACT.Identity,
+                             scale=T.wx[:, 32 * h + j:32 * h + j + 1]), "tm%d_%d" % (j, h))
+
+        def add(j, h, first):
+            s0 = SL * (2 * j + h)
+            a = T.acc[:, SL * h:SL * h + 129]
+            wait(V, "tm%d_%d" % (j, h))
+            if first:
+                wait(V, "tmo%d" % h)
+                o0 = SL * (2 * rank + h)
+                inc(V.tensor_tensor(a, T.tmp[:, o0:o0 + 129], T.tmp[:, s0:s0 + 129], ALU.add), "ac%d" % h)
+            else:
+                wait(V, "ac%d" % h)
+                inc(V.tensor_tensor(a, a, T.tmp[:, s0:s0 + 129], ALU.add), "ac%d" % h)
+
+        def divide(h):
+            wait(V, "ac%d" % h)
+            inc(V.reciprocal(T.rdn[:, h:h + 1], T.acc[:, SL * h + 128:SL * h + 129]), "rc%d" % h)
+            wait(V, "rc%d" % h)
+            inc(V.tensor_scalar(T.Z[:, 128 * h:128 * h + 128], T.acc[:, SL * h:SL * h + 128], T.rdn[:, h:h + 1], None, ALU.mult),
+                "z%d" % h)
+            wait(V, "z%d" % h)
+            inc(V.transpose(T.Zt[:, 128 * h:128 * h + 128], T.Z[:, 128 * h:128 * h + 128]), "zt%d" % h)
+
+        def blocks(h, nv):
+            k = 0
+            wait(V, "zt%d" % h)
+            wait(S, "zt%d" % h)
+            for a in range(4):
+                for d in range(4):
+                    out = T.O[32 * d:32 * d + 32, 128 * h + 32 * a:128 * h + 32 * a + 32]
+                    in_ = T.Zt[32 * a:32 * a + 32, 128 * h + 32 * d:128 * h + 32 * d + 32]
+                    if k < nv:
+                        inc(vcopy(out, in_), "cpv%d" % h)
+                    else:
+                        inc(scopy(out, in_), "cps%d" % h)
+                    k += 1
+            if nv:
+                wait(SY, "cpv%d" % h)
+            wait(SY, "cps%d" % h)
+            inc(SY.dma_start(T.o[:, 128 * h:128 * h + 128], T.O[:, 128 * h:128 * h + 128]), "outo", 16)
+
+        for i, j in enumerate(proc[:-1]):
+            for h in range(2):
+                weigh(j, h)
+                add(j, h, i == 0)
+        last = proc[-1]
+        weigh(last, 0)
+        weigh(last, 1)
+        add(last, 0, False)
+        divide(0)
+        blocks(0, 0)
+        add(last, 1, False)
+        divide(1)
+        blocks(1, 10)
+
+    g.wait_ge(sem.sent, nsent)
+    for name in sorted(tot):
+        if seen.get(name, 0) < tot[name]:
+            wait(g, name)

@@ -2,8 +2,7 @@ import numpy as np
 from concourse.mybir import dt, AluOpType, AxisListType, ActivationFunctionType
 
 N = 8
-MODE = "direct"
-NCH = 1
+NCH = 2
 SL = 132
 F32, BF, CODE, U8 = "float32", "bfloat16", "float8_e4m3fn_x4", "uint8"
 
@@ -13,9 +12,9 @@ SCRATCH = {
     "vo": ("sbuf", [128, 256], CODE), "vos": ("sbuf", [128, 256], U8),
     "onet": ("sbuf", [128, 512], BF), "atile": ("sbuf", [128, 128], F32),
     "n20": ("sbuf", [128, 1], F32), "e20": ("sbuf", [128, 1], BF),
-    "mT": ("sbuf", [128, 2], F32), "cT": ("sbuf", [128, 2], F32),
+    "mT": ("sbuf", [128, 8], F32), "craw": ("sbuf", [128, 4 * N], F32),
     "E": ("sbuf", [128, 256], F32), "C": ("sbuf", [128, 256], F32),
-    "SA": ("sbuf", [128, 1024], F32), "X": ("sbuf", [128, 1024], F32),
+    "crow": ("sbuf", [128, 256], F32), "X": ("sbuf", [128, 1024], F32),
     "P": ("sbuf", [128, 1024], BF), "pc": ("sbuf", [128, 256], CODE), "psc": ("sbuf", [128, 256], U8),
     "msg": ("sbuf", [128, 2 * SL], F32), "zw": ("sbuf", [128, 256], F32),
     "cland": ("sbuf", [128, 4 * N], F32), "negM": ("sbuf", [128, 2], F32),
@@ -27,11 +26,12 @@ SCRATCH = {
 }
 
 SEMAPHORES = (
-    ["ldq", "ldk", "m_one", "m_at", "m_n20", "m_wx", "m_zw", "qone", "e20s", "qq", "tr", "ct", "sent",
+    ["ldk", "m_one", "m_at", "m_n20", "m_wx", "m_zw", "qone", "e20s", "ct", "cown", "cr", "sent",
      "outc", "outp", "outw", "outo", "qarr0", "qarr1", "carr", "ng", "wxs", "wt"]
-    + ["%s%d" % (n, h) for n in ("st", "rd", "xp", "ex", "cl", "qp", "al", "ev", "tmo", "ac", "rc", "z", "zt", "cpv", "cps")
+    + ["%s%d" % (n, h) for n in ("ldq", "qq", "tr", "st", "rd", "xp", "ex", "cl", "qp", "al", "ev", "tmo", "ac", "rc", "z", "zt",
+                                 "cpv", "cps")
        for h in range(2)]
-    + ["%s%d" % (n, b) for n in ("sb", "sa") for b in range(4)]
+    + ["sb%d" % b for b in range(4)]
     + ["%s_%d%s" % (n, h, s) for n in ("s1", "s2") for h in range(2) for s in ("l", "h")]
     + ["x%d%d" % (h, b) for h in range(2) for b in range(4)]
     + ["%s%d_%d" % (n, j, h) for n in ("ar", "tm") for j in range(N) for h in range(2)]
@@ -87,25 +87,8 @@ def rank_program(g, core, T, topo):
         return m
     mine = [r for r in off if topo.die(T.cores[r]) == topo.die(rootc)]
     his = [r for r in off if r not in mine]
-    if MODE == "direct":
-        plan = {root: off[:1] + near + off[1:]}
-        proc = near + off
-    elif MODE == "two":
-        plan = {root: near[:1] + mine, near[0]: his}
-        proc = near + [r for pair in zip(mine, his) for r in pair]
-    else:
-        plan = {root: near[:1] + [r for r in mine if far(rootc, T.cores[r]) == 1]}
-        for r in mine:
-            if far(rootc, T.cores[r]) == 2:
-                up = [x for x in mine if far(rootc, T.cores[x]) == 1 and topo.same_plane(T.cores[x], T.cores[r])][0]
-                plan[up] = plan.get(up, []) + [r]
-        for r in his:
-            if far(rootc, T.cores[r]) == 2:
-                plan[near[0]] = plan.get(near[0], []) + [r]
-            else:
-                up = [x for x in mine if same_chip(T.cores[x], T.cores[r])][0]
-                plan[up] = plan.get(up, []) + [r]
-        proc = near + [r for r in off if far(rootc, T.cores[r]) == 1] + [r for r in off if far(rootc, T.cores[r]) == 2]
+    plan = {root: near[:1] + mine, near[0]: his}
+    proc = near + [r for pair in zip(mine, his) for r in pair]
     parent = {}
     for a in plan:
         for r in plan[a]:
@@ -119,15 +102,17 @@ def rank_program(g, core, T, topo):
         return S.activation(out, in_, ACT.Identity)
 
     if is_root:
-        inc(SY.dma_start(T.qt[:], T.q[:]), "ldq", 16)
-        wait(SY, "ldq")
+        inc(SY.dma_start(T.qt[:, 0:512], T.q[:, 0:512]), "ldq0", 16)
+        inc(S.dma_start(T.qt[:, 512:1024], T.q[:, 512:1024]), "ldq1", 16)
+        wait(SY, "ldq0")
+        wait(SY, "ldq1")
     inc(SY.dma_start(T.kcb[:].bitcast(u8), T.kc[:]), "ldk", 16)
     inc(SY.dma_start(T.ksb[:], T.ks[:]), "ldk", 16)
     inc(SY.dma_start(T.vo[:, 0:128].bitcast(u8), T.vc[:]), "ldk", 16)
     inc(SY.dma_start(T.vos[:, 0:128], T.vs[:]), "ldk", 16)
 
     inc(V.memset(T.onet[:], 1.0), "m_one")
-    inc(V.memset(T.atile[:], A), "m_at")
+    inc(V.memset(T.atile[:], 1.0), "m_at")
     inc(V.memset(T.n20[:], -20.0), "m_n20")
     if is_root:
         inc(V.memset(T.wx[:], 0.0), "m_wx")
@@ -142,17 +127,21 @@ def rank_program(g, core, T, topo):
 
     nsent = 0
     if is_root:
-        wait(V, "ldq")
-        inc(V.quantize_mx(T.qc[:], T.qs[:], T.qt[:]), "qq")
-        wait(g, "qq")
+        for k in range(2):
+            wait(V, "ldq%d" % k)
+            inc(V.quantize_mx(T.qc[:, 128 * k:128 * k + 128], T.qs[:, 128 * k:128 * k + 128], T.qt[:, 512 * k:512 * k + 512]),
+                "qq%d" % k)
     nq = 0 if is_root else 2 * engines(qmask(parent[rank], rank))
-    got = [is_root] * NCH
+    got = [False] * NCH
     for r in plan.get(rank, []):
         qrid, qpid = topo.addr(T.cores[r], core)
         m = qmask(rank, r)
         for k in range(NCH):
             if not got[k]:
-                g.wait_ge(sem["qarr%d" % k], nq)
+                if is_root:
+                    wait(g, "qq%d" % k)
+                else:
+                    g.wait_ge(sem["qarr%d" % k], nq)
                 got[k] = True
             cs = slice(CW * k, CW * k + CW)
             g.remote_dma(out_ap=T.qc[:, cs].bitcast(u8), in_ap=T.qc[:, cs].bitcast(u8), remote_sem=sem["qarr%d" % k],
@@ -162,41 +151,38 @@ def rank_program(g, core, T, topo):
             nsent += 2 * engines(m)
 
     wait(PE, "ldk")
-    if is_root:
-        wait(PE, "qq")
     for h in range(2):
-        if not is_root and (h == 0 or NCH == 2):
-            PE.wait_ge(sem["qarr%d" % (h if NCH == 2 else 0)], nq)
+        if is_root:
+            wait(PE, "qq%d" % h)
+        else:
+            PE.wait_ge(sem["qarr%d" % h], nq)
         inc(PE.matmul_mx(T.ps[:, 512 * h:512 * h + 512], T.qc[:, 128 * h:128 * h + 128], T.qs[:, 128 * h:128 * h + 128],
                          T.kcb[:], T.ksb[:], True, True), "st%d" % h)
     for b in range(4):
         inc(PE.matmul_mx(T.ps[:, 1024 + 512 * b:1024 + 512 * b + 256], T.kcb[:, 128 * b:128 * b + 128],
                          T.ksb[:, 128 * b:128 * b + 128], T.qc[:], T.qs[:], True, True), "sb%d" % b)
 
-    def scale(b):
-        wait(S, "sb%d" % b)
-        inc(S.activation(T.SA[:, 256 * b:256 * b + 256], T.ps[:, 1024 + 512 * b:1024 + 512 * b + 256], ACT.Identity, scale=A),
-            "sa%d" % b)
+    rid, pid = (None, None) if is_root else topo.addr(rootc, core)
+    mk = 0 if is_root else topo.mask(core, rootc)
 
-    wait(V, "st0")
-    inc(V.tensor_reduce(T.mT[:, 0:1], T.ps[:, 0:512], AX.X, ALU.max), "rd0")
-    wait(S, "rd0")
-    wait(S, "m_at")
-    inc(S.activation(T.E[:, 0:128], T.atile[:], ACT.Identity, scale=T.mT[:, 0:1]), "xp0")
-    wait(V, "st1")
-    inc(V.tensor_reduce(T.mT[:, 1:2], T.ps[:, 512:1024], AX.X, ALU.max), "rd1")
-    wait(V, "rd1")
-    wait(V, "m_at")
-    inc(V.tensor_scalar(T.E[:, 128:256], T.atile[:], T.mT[:, 1:2], None, ALU.mult), "xp1")
-    scale(0)
-    scale(1)
-    wait(V, "xp0")
-    wait(V, "xp1")
-    inc(V.transpose(T.C[:], T.E[:]), "tr")
+    def largest(h):
+        wait(V, "st%d" % h)
+        inc(V.tensor_reduce(T.mT[:, 4 * h:4 * h + 1], T.ps[:, 512 * h:512 * h + 512], AX.X, ALU.max), "rd%d" % h)
+        if not is_root:
+            wait(g, "rd%d" % h)
+            g.remote_dma(out_ap=T.craw[:, 4 * rank + h:4 * rank + h + 1], in_ap=T.mT[:, 4 * h:4 * h + 1], remote_sem=sem.carr,
+                         local_sem=sem.sent, pid=pid, routing_id=rid, dma_engine_mask=mk)
+        wait(S, "rd%d" % h)
+        wait(S, "m_at")
+        inc(S.activation(T.E[:, 128 * h:128 * h + 128], T.atile[:], ACT.Identity, scale=T.mT[:, 4 * h:4 * h + 1]), "xp%d" % h)
+
+    def turn(h):
+        wait(V, "xp%d" % h)
+        inc(V.transpose(T.C[:, 128 * h:128 * h + 128], T.E[:, 128 * h:128 * h + 128]), "tr%d" % h)
 
     def spread(q, copy, h, s):
         lo = 0 if s == "l" else 2
-        wait(q, "tr")
+        wait(q, "tr%d" % h)
         for a in (lo, lo + 1):
             o = lo + 1 if a == lo else lo
             c0 = 128 * h + 32 * a
@@ -206,37 +192,16 @@ def rank_program(g, core, T, topo):
         src, dst = (0, 64) if s == "l" else (64, 0)
         inc(copy(T.C[dst:dst + 64, c0:c0 + 64], T.C[src:src + 64, c0:c0 + 64]), "s2_%d%s" % (h, s))
 
-    spread(V, vcopy, 0, "l")
-    spread(S, scopy, 0, "h")
-    scale(2)
-    spread(S, scopy, 1, "l")
-    spread(S, scopy, 1, "h")
-    scale(3)
-    wait(S, "rd1")
-    cdst = T.cland[:, 4 * rank:4 * rank + 2] if is_root else T.cT[:]
-    inc(S.activation(cdst, T.mT[:], ACT.Identity, scale=A), "ct")
-    for h in range(2):
-        for s in ("l", "h"):
-            wait(SY, "s2_%d%s" % (h, s))
-    inc(SY.dma_start(T.c[:], T.C[0:1, :]), "outc", 16)
-
-    rid, pid = (None, None) if is_root else topo.addr(rootc, core)
-    mk = 0 if is_root else topo.mask(core, rootc)
-    if not is_root:
-        wait(g, "ct")
-        g.remote_dma(out_ap=T.cland[:, 4 * rank:4 * rank + 2], in_ap=T.cT[:], remote_sem=sem.carr, local_sem=sem.sent,
-                     pid=pid, routing_id=rid, dma_engine_mask=mk)
-        nsent += engines(mk)
-
     def sub_exp(h, b):
         c0 = 256 * b + 128 * h
-        wait(V, "sa%d" % b)
+        s0 = 1024 + 512 * b + 128 * h
+        wait(V, "sb%d" % b)
         wait(V, "s2_%dl" % h)
         wait(V, "s2_%dh" % h)
-        inc(V.tensor_tensor(T.X[:, c0:c0 + 128], T.SA[:, c0:c0 + 128], T.C[:, 128 * h:128 * h + 128], ALU.subtract),
+        inc(V.tensor_tensor(T.X[:, c0:c0 + 128], T.ps[:, s0:s0 + 128], T.C[:, 128 * h:128 * h + 128], ALU.subtract),
             "x%d%d" % (h, b))
         wait(S, "x%d%d" % (h, b))
-        inc(S.activation(T.P[:, 512 * h + b:512 * h + 512:4], T.X[:, c0:c0 + 128], ACT.Exp), "ex%d" % h)
+        inc(S.activation(T.P[:, 512 * h + b:512 * h + 512:4], T.X[:, c0:c0 + 128], ACT.Exp, scale=A), "ex%d" % h)
 
     def finish(h):
         wait(V, "ex%d" % h)
@@ -261,23 +226,45 @@ def rank_program(g, core, T, topo):
         g.remote_dma(out_ap=T.aland[:, s0:s0 + 129], in_ap=T.msg[:, SL * h:SL * h + 129], remote_sem=sem["ar%d_%d" % (rank, h)],
                      local_sem=sem.sent, pid=pid, routing_id=rid, dma_engine_mask=mk)
 
-    for h, b in ((0, 0), (0, 1), (0, 2), (1, 0), (0, 3), (1, 1)):
+    largest(0)
+    turn(0)
+    spread(V, vcopy, 0, "l")
+    spread(S, scopy, 0, "h")
+    largest(1)
+    sub_exp(0, 0)
+    turn(1)
+    spread(S, scopy, 1, "l")
+    spread(S, scopy, 1, "h")
+    if is_root:
+        for h in range(2):
+            inc(scopy(T.craw[:, 4 * rank + h:4 * rank + h + 1], T.mT[:, 4 * h:4 * h + 1]), "cown")
+    else:
+        nsent += 2 * engines(mk)
+    for h, b in ((0, 1), (0, 2), (0, 3), (1, 0), (1, 1), (1, 2)):
         sub_exp(h, b)
     finish(0)
-    sub_exp(1, 2)
+    sub_exp(1, 3)
     if not is_root:
         ship(0)
-    sub_exp(1, 3)
     finish(1)
     if not is_root:
         ship(1)
         nsent += 2 * engines(mk)
+    for h in range(2):
+        for s in ("l", "h"):
+            wait(S, "s2_%d%s" % (h, s))
+    inc(S.activation(T.crow[0:1, :], T.C[0:1, :], ACT.Identity, scale=A), "cr")
+    wait(SY, "cr")
+    inc(SY.dma_start(T.c[:], T.crow[0:1, :]), "outc", 16)
 
     if is_root:
         ncarr = 0
         for r in others:
-            ncarr += engines(topo.mask(T.cores[r], rootc))
-        V.wait_ge(sem.carr, ncarr)
+            ncarr += 2 * engines(topo.mask(T.cores[r], rootc))
+        S.wait_ge(sem.carr, ncarr)
+        wait(S, "cown")
+        for h in range(2):
+            inc(S.activation(T.cland[:, h:4 * N:4], T.craw[:, h:4 * N:4], ACT.Identity, scale=A), "ct")
         wait(V, "ct")
         for h in range(2):
             inc(V.tensor_reduce(T.negM[:, h:h + 1], T.cland[:, h:4 * N:4], AX.X, ALU.max, negate=True), "ng")

@@ -1,4 +1,5 @@
 import numpy as np
+from concourse.bass import DstId, RemoteDMATransfer
 from concourse.mybir import dt, AluOpType, AxisListType, ActivationFunctionType
 
 N = 8
@@ -26,22 +27,20 @@ SCRATCH = {
 }
 
 SEMAPHORES = (
-    ["ldk", "m_one", "m_at", "m_n20", "m_wx", "m_zw", "qone", "e20s", "ct", "cown", "cr", "sent",
-     "outc", "outp", "outw", "outo", "qarr0", "qarr1", "carr", "ng", "wxs", "wt"]
-    + ["%s%d" % (n, h) for n in ("ldq", "qq", "tr", "st", "rd", "xp", "ex", "cl", "qp", "al", "ev", "tmo", "ac", "rc", "z", "zt",
+    ["ldk", "ldv", "m_one", "m_at", "m_n20", "m_wx", "m_zw", "qone", "e20s", "ct", "cown", "cr", "sent", "sent0",
+     "outc", "outp", "outw", "outo", "qarr0", "qarr1", "onearr", "carr", "ng", "wxs", "wt"]
+    + ["%s%d" % (n, h) for n in ("ldq", "qq", "tr", "st", "rd", "xp", "cl", "qp", "al", "ev", "tmo", "ac", "rc", "z", "zt",
                                  "cpv", "cps")
        for h in range(2)]
     + ["sb%d" % b for b in range(4)]
     + ["%s_%d%s" % (n, h, s) for n in ("s1", "s2") for h in range(2) for s in ("l", "h")]
-    + ["x%d%d" % (h, b) for h in range(2) for b in range(4)]
+    + ["%s%d%d" % (n, h, b) for n in ("x", "ex") for h in range(2) for b in range(4)]
     + ["%s%d_%d" % (n, j, h) for n in ("ar", "tm") for j in range(N) for h in range(2)]
 )
 
 
 def rank_program(g, core, T, topo):
     rank = T.rank_of(core)
-    if rank is None:
-        return
     sem = T.sem
     root = T.root
     rootc = T.cores[root]
@@ -80,20 +79,85 @@ def rank_program(g, core, T, topo):
     for r in off:
         leave |= topo.mask(rootc, T.cores[r])
 
-    def qmask(a, r):
-        m = topo.mask(T.cores[a], T.cores[r])
-        if same_chip(T.cores[a], T.cores[r]) and (m & ~leave):
+    def qmask(a, b):
+        m = topo.mask(a, b)
+        if same_chip(a, b) and (m & ~leave):
             m &= ~leave
         return m
-    mine = [r for r in off if topo.die(T.cores[r]) == topo.die(rootc)]
-    his = [r for r in off if r not in mine]
-    plan = {root: near[:1] + mine, near[0]: his}
-    proc = near + [r for pair in zip(mine, his) for r in pair]
-    parent = {}
+    nearc = T.cores[near[0]]
+    spare = [c for c in range(max(T.cores) + 1) if same_chip(c, rootc) and T.rank_of(c) is None]
+    plan, oplan, helpers, order = {}, {}, [], []
+    for s_ in (rootc, nearc):
+        D = [T.cores[r] for r in off if topo.die(T.cores[r]) == topo.die(s_)]
+        sw = [d for d in D if topo.same_plane(s_, d)]
+        hs = [c for c in spare if topo.die(c) == topo.die(s_) and all(topo.may_write(c, d) for d in D)]
+        if sw and hs:
+            rest = [d for d in D if d != sw[0]]
+            plan[hs[-1]] = [sw[0]]
+            oplan[hs[-1]] = [sw[0]] + rest[1:]
+            helpers.append(hs[-1])
+            plan[s_] = rest
+            oplan[s_] = rest[:1]
+            order.append(rest[:1] + [sw[0]] + rest[1:])
+        else:
+            plan[s_] = D
+            oplan[s_] = D
+            order.append(D)
+    proc = near + [T.rank_of(d) for pair in zip(*order) for d in pair]
+    parent, oparent = {nearc: rootc}, {}
+    for c in helpers:
+        parent[c] = rootc
     for a in plan:
-        for r in plan[a]:
-            parent[r] = a
-    CW = 256 // NCH
+        for d in plan[a]:
+            parent[d] = a
+        for d in oplan[a]:
+            oparent[d] = a
+    if rank is None and core not in plan:
+        return
+    sentn = [0]
+
+    def xfer(buf, cs, code, dests, m, name, cnt=sentn):
+        def ap():
+            return buf[:, cs].bitcast(u8) if code else buf[:, cs]
+        ids = []
+        for d in dests:
+            r_, p_ = topo.addr(d, core)
+            ids.append(DstId(rid=r_, pnc=p_))
+        cnt[0] += engines(m)
+        return RemoteDMATransfer(dst_ids=ids, dma_engine_mask=m, remote_sem=sem[name], srcs=[ap()], dsts=[ap() for d in dests])
+
+    def make_one():
+        inc(V.memset(T.onet[:], 1.0), "m_one")
+        wait(V, "m_one")
+        inc(V.quantize_mx(T.vo[:, 128:256], T.vos[:, 128:256], T.onet[:]), "qone")
+
+    def send_one():
+        m = 0
+        for d in oplan[core]:
+            m = topo.mask(core, d) if not m else m & topo.mask(core, d)
+        wait(g, "qone")
+        g.remote_dma_fused([xfer(T.vo, slice(128, 130), True, oplan[core], m, "onearr")], local_sem=sem.sent)
+        g.remote_dma_fused([xfer(T.vos, slice(128, 130), False, oplan[core], m, "onearr")], local_sem=sem.sent)
+
+    def pass_on():
+        n_ = 2 * engines(qmask(parent[core], core))
+        got_ = [False] * NCH
+        for d in plan[core]:
+            m = qmask(core, d)
+            for k in range(NCH):
+                if not got_[k]:
+                    g.wait_ge(sem["qarr%d" % k], n_)
+                    got_[k] = True
+                cs = slice(128 * k, 128 * k + 128)
+                g.remote_dma_fused([xfer(T.qc, cs, True, [d], m, "qarr%d" % k)], local_sem=sem.sent)
+                g.remote_dma_fused([xfer(T.qs, cs, False, [d], m, "qarr%d" % k)], local_sem=sem.sent)
+
+    if rank is None:
+        make_one()
+        send_one()
+        pass_on()
+        g.wait_ge(sem.sent, sentn[0])
+        return
 
     def vcopy(out, in_):
         return V.tensor_copy(out, in_)
@@ -104,14 +168,18 @@ def rank_program(g, core, T, topo):
     if is_root:
         inc(SY.dma_start(T.qt[:, 0:512], T.q[:, 0:512]), "ldq0", 16)
         inc(S.dma_start(T.qt[:, 512:1024], T.q[:, 512:1024]), "ldq1", 16)
-        wait(SY, "ldq0")
-        wait(SY, "ldq1")
-    inc(SY.dma_start(T.kcb[:].bitcast(u8), T.kc[:]), "ldk", 16)
-    inc(SY.dma_start(T.ksb[:], T.ks[:]), "ldk", 16)
-    inc(SY.dma_start(T.vo[:, 0:128].bitcast(u8), T.vc[:]), "ldk", 16)
-    inc(SY.dma_start(T.vos[:, 0:128], T.vs[:]), "ldk", 16)
 
-    inc(V.memset(T.onet[:], 1.0), "m_one")
+    def load_kv():
+        inc(SY.dma_start(T.kcb[:].bitcast(u8), T.kc[:]), "ldk", 16)
+        inc(SY.dma_start(T.ksb[:], T.ks[:]), "ldk", 16)
+        inc(SY.dma_start(T.vo[:, 0:128].bitcast(u8), T.vc[:]), "ldv", 16)
+        inc(SY.dma_start(T.vos[:, 0:128], T.vs[:]), "ldv", 16)
+    if not is_root:
+        load_kv()
+
+    if core in plan:
+        make_one()
+        send_one()
     inc(V.memset(T.atile[:], 1.0), "m_at")
     inc(V.memset(T.n20[:], -20.0), "m_n20")
     if is_root:
@@ -120,8 +188,6 @@ def rank_program(g, core, T, topo):
         inc(V.memset(T.zw[0:8, :], 0.0), "m_zw")
         wait(SY, "m_zw")
         inc(SY.dma_start(T.w[:], T.zw[0:8, :]), "outw", 16)
-    wait(V, "m_one")
-    inc(V.quantize_mx(T.vo[:, 128:256], T.vos[:, 128:256], T.onet[:]), "qone")
     wait(S, "m_n20")
     inc(S.activation(T.e20[:], T.n20[:], ACT.Exp), "e20s")
 
@@ -131,24 +197,26 @@ def rank_program(g, core, T, topo):
             wait(V, "ldq%d" % k)
             inc(V.quantize_mx(T.qc[:, 128 * k:128 * k + 128], T.qs[:, 128 * k:128 * k + 128], T.qt[:, 512 * k:512 * k + 512]),
                 "qq%d" % k)
-    nq = 0 if is_root else 2 * engines(qmask(parent[rank], rank))
-    got = [False] * NCH
-    for r in plan.get(rank, []):
-        qrid, qpid = topo.addr(T.cores[r], core)
-        m = qmask(rank, r)
-        for k in range(NCH):
-            if not got[k]:
-                if is_root:
+    nq = 0 if is_root else 2 * engines(qmask(parent[core], core))
+    if is_root:
+        on = [([nearc], 0), ([nearc], 1)] + ([(helpers, 0), (helpers, 1)] if helpers else [])
+        out = [([d], k) for d in plan[core] for k in range(NCH)]
+        got = [False] * NCH
+        first = [0]
+        for i in range(max(len(on), len(out))):
+            both = on[i:i + 1] + out[i:i + 1]
+            for ds, k in both:
+                if not got[k]:
                     wait(g, "qq%d" % k)
-                else:
-                    g.wait_ge(sem["qarr%d" % k], nq)
-                got[k] = True
-            cs = slice(CW * k, CW * k + CW)
-            g.remote_dma(out_ap=T.qc[:, cs].bitcast(u8), in_ap=T.qc[:, cs].bitcast(u8), remote_sem=sem["qarr%d" % k],
-                         local_sem=sem.sent, pid=qpid, routing_id=qrid, dma_engine_mask=m)
-            g.remote_dma(out_ap=T.qs[:, cs], in_ap=T.qs[:, cs], remote_sem=sem["qarr%d" % k], local_sem=sem.sent,
-                         pid=qpid, routing_id=qrid, dma_engine_mask=m)
-            nsent += 2 * engines(m)
+                    got[k] = True
+            for buf, code in ((T.qc, True), (T.qs, False)):
+                g.remote_dma_fused([xfer(buf, slice(128 * k, 128 * k + 128), code, ds, qmask(core, ds[0]), "qarr%d" % k,
+                                         first if i < NCH else sentn) for ds, k in both],
+                                   local_sem=sem.sent0 if i < NCH else sem.sent)
+        SY.wait_ge(sem.sent0, first[0])
+        load_kv()
+    elif core in plan:
+        pass_on()
 
     wait(PE, "ldk")
     for h in range(2):
@@ -201,22 +269,34 @@ def rank_program(g, core, T, topo):
         inc(V.tensor_tensor(T.X[:, c0:c0 + 128], T.ps[:, s0:s0 + 128], T.C[:, 128 * h:128 * h + 128], ALU.subtract),
             "x%d%d" % (h, b))
         wait(S, "x%d%d" % (h, b))
-        inc(S.activation(T.P[:, 512 * h + b:512 * h + 512:4], T.X[:, c0:c0 + 128], ACT.Exp, scale=A), "ex%d" % h)
+        inc(S.activation(T.P[:, 512 * h + b:512 * h + 512:4], T.X[:, c0:c0 + 128], ACT.Exp, scale=A), "ex%d%d" % (h, b))
 
-    def finish(h):
-        wait(V, "ex%d" % h)
+    def finish(h, quarters):
         wait(V, "e20s")
-        inc(V.tensor_scalar(T.P[:, 512 * h:512 * h + 512], T.P[:, 512 * h:512 * h + 512], T.e20[:, 0:1], None, ALU.max),
-            "cl%d" % h)
+        if quarters:
+            for b in range(4):
+                wait(V, "ex%d%d" % (h, b))
+                v = T.P[:, 512 * h + b:512 * h + 512:4]
+                inc(V.tensor_scalar(v, v, T.e20[:, 0:1], None, ALU.max), "cl%d" % h)
+        else:
+            for b in range(4):
+                wait(V, "ex%d%d" % (h, b))
+            inc(V.tensor_scalar(T.P[:, 512 * h:512 * h + 512], T.P[:, 512 * h:512 * h + 512], T.e20[:, 0:1], None, ALU.max),
+                "cl%d" % h)
         wait(V, "cl%d" % h)
         inc(V.quantize_mx(T.pc[:, 128 * h:128 * h + 128], T.psc[:, 128 * h:128 * h + 128], T.P[:, 512 * h:512 * h + 512]),
             "qp%d" % h)
-        wait(SY, "cl%d" % h)
-        inc(SY.dma_start(T.p[:, 512 * h:512 * h + 512], T.P[:, 512 * h:512 * h + 512]), "outp", 16)
+        if is_root:
+            wait(SY, "cl%d" % h)
+            inc(SY.dma_start(T.p[:, 512 * h:512 * h + 512], T.P[:, 512 * h:512 * h + 512]), "outp", 16)
         wait(PE, "qp%d" % h)
-        wait(PE, "qone")
-        inc(PE.matmul_mx(T.ps[:, 3072 + 512 * h:3072 + 512 * h + 256], T.pc[:, 128 * h:128 * h + 128],
-                         T.psc[:, 128 * h:128 * h + 128], T.vo[:], T.vos[:], True, True), "al%d" % h)
+        wait(PE, "ldv")
+        if core in plan:
+            wait(PE, "qone")
+        else:
+            PE.wait_ge(sem.onearr, 2 * engines(topo.mask(oparent[core], core)))
+        inc(PE.matmul_mx(T.ps[:, 3072 + 512 * h:3072 + 512 * h + 130], T.pc[:, 128 * h:128 * h + 128],
+                         T.psc[:, 128 * h:128 * h + 128], T.vo[:, 0:130], T.vos[:, 0:130], True, True), "al%d" % h)
 
     def ship(h):
         wait(S, "al%d" % h)
@@ -242,14 +322,18 @@ def rank_program(g, core, T, topo):
         nsent += 2 * engines(mk)
     for h, b in ((0, 1), (0, 2), (0, 3), (1, 0), (1, 1), (1, 2)):
         sub_exp(h, b)
-    finish(0)
+    finish(0, False)
     sub_exp(1, 3)
     if not is_root:
         ship(0)
-    finish(1)
+    finish(1, True)
     if not is_root:
         ship(1)
         nsent += 2 * engines(mk)
+        SY.wait_ge(sem.sent, nsent + sentn[0])
+        wait(SY, "cl0")
+        wait(SY, "cl1")
+        inc(SY.dma_start(T.p[:], T.P[:]), "outp", 16)
     for h in range(2):
         for s in ("l", "h"):
             wait(S, "s2_%d%s" % (h, s))
@@ -345,7 +429,7 @@ def rank_program(g, core, T, topo):
         divide(1)
         blocks(1, 10)
 
-    g.wait_ge(sem.sent, nsent)
+    g.wait_ge(sem.sent, nsent + sentn[0])
     for name in sorted(tot):
         if seen.get(name, 0) < tot[name]:
             wait(g, name)

import numpy as np
from concourse.bass import DstId, RemoteDMATransfer
from concourse.mybir import dt, AluOpType, AxisListType, ActivationFunctionType

N = 8
NCH = 2
SL = 132
F32, BF, CODE, U8 = "float32", "bfloat16", "float8_e4m3fn_x4", "uint8"

SCRATCH = {
    "qt": ("sbuf", [128, 1024], BF), "qc": ("sbuf", [128, 256], CODE), "qs": ("sbuf", [128, 256], U8),
    "kcb": ("sbuf", [128, 512], CODE), "ksb": ("sbuf", [128, 512], U8),
    "vo": ("sbuf", [128, 256], CODE), "vos": ("sbuf", [128, 256], U8),
    "onet": ("sbuf", [128, 512], BF), "atile": ("sbuf", [128, 128], F32),
    "n20": ("sbuf", [128, 1], F32), "e20": ("sbuf", [128, 1], BF),
    "mT": ("sbuf", [128, 8], F32), "craw": ("sbuf", [128, 4 * N], F32),
    "E": ("sbuf", [128, 256], F32), "C": ("sbuf", [128, 256], F32),
    "crow": ("sbuf", [128, 256], F32), "X": ("sbuf", [128, 1024], F32),
    "P": ("sbuf", [128, 1024], BF), "pc": ("sbuf", [128, 256], CODE), "psc": ("sbuf", [128, 256], U8),
    "msg": ("sbuf", [128, 2 * SL], F32), "zw": ("sbuf", [128, 256], F32),
    "cland": ("sbuf", [128, 4 * N], F32), "negM": ("sbuf", [128, 2], F32),
    "wx": ("sbuf", [128, 64], F32), "wxt": ("sbuf", [128, 64], F32),
    "aland": ("sbuf", [128, 2 * N * SL], F32), "tmp": ("sbuf", [128, 2 * N * SL], F32),
    "acc": ("sbuf", [128, 2 * SL], F32), "rdn": ("sbuf", [128, 2], F32),
    "Z": ("sbuf", [128, 256], F32), "Zt": ("sbuf", [128, 256], F32), "O": ("sbuf", [128, 256], F32),
    "ps": ("psum", [128, 4096], F32),
}

SEMAPHORES = (
    ["ldk", "ldv", "m_one", "m_at", "m_n20", "m_wx", "m_zw", "qone", "e20s", "ct", "cown", "cr", "sent", "sent0",
     "outc", "outp", "outw", "outo", "qarr0", "qarr1", "onearr", "carr", "ng", "wxs", "wt"]
    + ["%s%d" % (n, h) for n in ("ldq", "qq", "tr", "st", "rd", "xp", "cl", "qp", "al", "ev", "tmo", "ac", "rc", "z", "zt",
                                 "cpv", "cps")
       for h in range(2)]
    + ["sb%d" % b for b in range(4)]
    + ["%s_%d%s" % (n, h, s) for n in ("s1", "s2") for h in range(2) for s in ("l", "h")]
    + ["%s%d%d" % (n, h, b) for n in ("x", "ex") for h in range(2) for b in range(4)]
    + ["%s%d_%d" % (n, j, h) for n in ("ar", "tm") for j in range(N) for h in range(2)]
)


def rank_program(g, core, T, topo):
    rank = T.rank_of(core)
    sem = T.sem
    root = T.root
    rootc = T.cores[root]
    is_root = rank == root
    V, S, PE, SY = g.vector, g.scalar, g.tensor, g.sync
    u8 = dt.uint8
    ALU, ACT, AX = AluOpType, ActivationFunctionType, AxisListType
    A = float(np.float32(0.0125))

    tot, seen = {}, {}

    def inc(ins, name, n=1):
        ins.then_inc(sem[name], n)
        tot[name] = tot.get(name, 0) + n

    def wait(q, name, n=None):
        n = tot[name] if n is None else n
        q.wait_ge(sem[name], n)
        seen[name] = max(seen.get(name, 0), n)

    def engines(m):
        return bin(m).count("1")

    def same_chip(a, b):
        return topo.host(a) == topo.host(b) and topo.chip(a) == topo.chip(b)

    def far(a, b):
        if same_chip(a, b):
            return 0
        return 1 if (topo.mates(a, b) or topo.same_plane(a, b)) else 2

    others = [r for r in range(N) if r != root]
    near = [r for r in others if same_chip(T.cores[r], rootc)]
    off = sorted([r for r in others if r not in near], key=lambda r: -far(rootc, T.cores[r]))
    leave = 0
    for r in off:
        leave |= topo.mask(rootc, T.cores[r])

    def qmask(a, b):
        m = topo.mask(a, b)
        if same_chip(a, b) and (m & ~leave):
            m &= ~leave
        return m
    nearc = T.cores[near[0]]
    spare = [c for c in range(max(T.cores) + 1) if same_chip(c, rootc) and T.rank_of(c) is None]
    plan, oplan, helpers, order = {}, {}, [], []
    for s_ in (rootc, nearc):
        D = [T.cores[r] for r in off if topo.die(T.cores[r]) == topo.die(s_)]
        sw = [d for d in D if topo.same_plane(s_, d)]
        hs = [c for c in spare if topo.die(c) == topo.die(s_) and all(topo.may_write(c, d) for d in D)]
        if sw and hs:
            rest = [d for d in D if d != sw[0]]
            plan[hs[-1]] = [sw[0]]
            oplan[hs[-1]] = [sw[0]] + rest[1:]
            helpers.append(hs[-1])
            plan[s_] = rest
            oplan[s_] = rest[:1]
            order.append(rest[:1] + [sw[0]] + rest[1:])
        else:
            plan[s_] = D
            oplan[s_] = D
            order.append(D)
    proc = near + [T.rank_of(d) for pair in zip(*order) for d in pair]
    parent, oparent = {nearc: rootc}, {}
    for c in helpers:
        parent[c] = rootc
    for a in plan:
        for d in plan[a]:
            parent[d] = a
        for d in oplan[a]:
            oparent[d] = a
    if rank is None and core not in plan:
        return
    sentn = [0]

    def xfer(buf, cs, code, dests, m, name, cnt=sentn):
        def ap():
            return buf[:, cs].bitcast(u8) if code else buf[:, cs]
        ids = []
        for d in dests:
            r_, p_ = topo.addr(d, core)
            ids.append(DstId(rid=r_, pnc=p_))
        cnt[0] += engines(m)
        return RemoteDMATransfer(dst_ids=ids, dma_engine_mask=m, remote_sem=sem[name], srcs=[ap()], dsts=[ap() for d in dests])

    def make_one():
        inc(V.memset(T.onet[:], 1.0), "m_one")
        wait(V, "m_one")
        inc(V.quantize_mx(T.vo[:, 128:256], T.vos[:, 128:256], T.onet[:]), "qone")

    def send_one():
        m = 0
        for d in oplan[core]:
            m = topo.mask(core, d) if not m else m & topo.mask(core, d)
        wait(g, "qone")
        g.remote_dma_fused([xfer(T.vo, slice(128, 130), True, oplan[core], m, "onearr")], local_sem=sem.sent)
        g.remote_dma_fused([xfer(T.vos, slice(128, 130), False, oplan[core], m, "onearr")], local_sem=sem.sent)

    def pass_on():
        n_ = 2 * engines(qmask(parent[core], core))
        got_ = [False] * NCH
        for d in plan[core]:
            m = qmask(core, d)
            for k in range(NCH):
                if not got_[k]:
                    g.wait_ge(sem["qarr%d" % k], n_)
                    got_[k] = True
                cs = slice(128 * k, 128 * k + 128)
                g.remote_dma_fused([xfer(T.qc, cs, True, [d], m, "qarr%d" % k)], local_sem=sem.sent)
                g.remote_dma_fused([xfer(T.qs, cs, False, [d], m, "qarr%d" % k)], local_sem=sem.sent)

    if rank is None:
        make_one()
        send_one()
        pass_on()
        g.wait_ge(sem.sent, sentn[0])
        return

    def vcopy(out, in_):
        return V.tensor_copy(out, in_)

    def scopy(out, in_):
        return S.activation(out, in_, ACT.Identity)

    if is_root:
        inc(SY.dma_start(T.qt[:, 0:512], T.q[:, 0:512]), "ldq0", 16)
        inc(S.dma_start(T.qt[:, 512:1024], T.q[:, 512:1024]), "ldq1", 16)

    def load_kv():
        inc(SY.dma_start(T.kcb[:].bitcast(u8), T.kc[:]), "ldk", 16)
        inc(SY.dma_start(T.ksb[:], T.ks[:]), "ldk", 16)
        inc(SY.dma_start(T.vo[:, 0:128].bitcast(u8), T.vc[:]), "ldv", 16)
        inc(SY.dma_start(T.vos[:, 0:128], T.vs[:]), "ldv", 16)
    if not is_root:
        load_kv()

    if core in plan:
        make_one()
        send_one()
    inc(V.memset(T.atile[:], 1.0), "m_at")
    inc(V.memset(T.n20[:], -20.0), "m_n20")
    if is_root:
        inc(V.memset(T.wx[:], 0.0), "m_wx")
    else:
        inc(V.memset(T.zw[0:8, :], 0.0), "m_zw")
        wait(SY, "m_zw")
        inc(SY.dma_start(T.w[:], T.zw[0:8, :]), "outw", 16)
    wait(S, "m_n20")
    inc(S.activation(T.e20[:], T.n20[:], ACT.Exp), "e20s")

    nsent = 0
    if is_root:
        for k in range(2):
            wait(V, "ldq%d" % k)
            inc(V.quantize_mx(T.qc[:, 128 * k:128 * k + 128], T.qs[:, 128 * k:128 * k + 128], T.qt[:, 512 * k:512 * k + 512]),
                "qq%d" % k)
    nq = 0 if is_root else 2 * engines(qmask(parent[core], core))
    if is_root:
        on = [([nearc], 0), ([nearc], 1)] + ([(helpers, 0), (helpers, 1)] if helpers else [])
        out = [([d], k) for d in plan[core] for k in range(NCH)]
        got = [False] * NCH
        first = [0]
        for i in range(max(len(on), len(out))):
            both = on[i:i + 1] + out[i:i + 1]
            for ds, k in both:
                if not got[k]:
                    wait(g, "qq%d" % k)
                    got[k] = True
            for buf, code in ((T.qc, True), (T.qs, False)):
                g.remote_dma_fused([xfer(buf, slice(128 * k, 128 * k + 128), code, ds, qmask(core, ds[0]), "qarr%d" % k,
                                         first if i < NCH else sentn) for ds, k in both],
                                   local_sem=sem.sent0 if i < NCH else sem.sent)
        SY.wait_ge(sem.sent0, first[0])
        load_kv()
    elif core in plan:
        pass_on()

    wait(PE, "ldk")
    for h in range(2):
        if is_root:
            wait(PE, "qq%d" % h)
        else:
            PE.wait_ge(sem["qarr%d" % h], nq)
        inc(PE.matmul_mx(T.ps[:, 512 * h:512 * h + 512], T.qc[:, 128 * h:128 * h + 128], T.qs[:, 128 * h:128 * h + 128],
                         T.kcb[:], T.ksb[:], True, True), "st%d" % h)
    for b in range(4):
        inc(PE.matmul_mx(T.ps[:, 1024 + 512 * b:1024 + 512 * b + 256], T.kcb[:, 128 * b:128 * b + 128],
                         T.ksb[:, 128 * b:128 * b + 128], T.qc[:], T.qs[:], True, True), "sb%d" % b)

    rid, pid = (None, None) if is_root else topo.addr(rootc, core)
    mk = 0 if is_root else topo.mask(core, rootc)

    def largest(h):
        wait(V, "st%d" % h)
        inc(V.tensor_reduce(T.mT[:, 4 * h:4 * h + 1], T.ps[:, 512 * h:512 * h + 512], AX.X, ALU.max), "rd%d" % h)
        if not is_root:
            wait(g, "rd%d" % h)
            g.remote_dma(out_ap=T.craw[:, 4 * rank + h:4 * rank + h + 1], in_ap=T.mT[:, 4 * h:4 * h + 1], remote_sem=sem.carr,
                         local_sem=sem.sent, pid=pid, routing_id=rid, dma_engine_mask=mk)
        wait(S, "rd%d" % h)
        wait(S, "m_at")
        inc(S.activation(T.E[:, 128 * h:128 * h + 128], T.atile[:], ACT.Identity, scale=T.mT[:, 4 * h:4 * h + 1]), "xp%d" % h)

    def turn(h):
        wait(V, "xp%d" % h)
        inc(V.transpose(T.C[:, 128 * h:128 * h + 128], T.E[:, 128 * h:128 * h + 128]), "tr%d" % h)

    def spread(q, copy, h, s):
        lo = 0 if s == "l" else 2
        wait(q, "tr%d" % h)
        for a in (lo, lo + 1):
            o = lo + 1 if a == lo else lo
            c0 = 128 * h + 32 * a
            inc(copy(T.C[32 * o:32 * o + 32, c0:c0 + 32], T.C[32 * a:32 * a + 32, c0:c0 + 32]), "s1_%d%s" % (h, s))
        wait(q, "s1_%d%s" % (h, s))
        c0 = 128 * h + 32 * lo
        src, dst = (0, 64) if s == "l" else (64, 0)
        inc(copy(T.C[dst:dst + 64, c0:c0 + 64], T.C[src:src + 64, c0:c0 + 64]), "s2_%d%s" % (h, s))

    def sub_exp(h, b):
        c0 = 256 * b + 128 * h
        s0 = 1024 + 512 * b + 128 * h
        wait(V, "sb%d" % b)
        wait(V, "s2_%dl" % h)
        wait(V, "s2_%dh" % h)
        inc(V.tensor_tensor(T.X[:, c0:c0 + 128], T.ps[:, s0:s0 + 128], T.C[:, 128 * h:128 * h + 128], ALU.subtract),
            "x%d%d" % (h, b))
        wait(S, "x%d%d" % (h, b))
        inc(S.activation(T.P[:, 512 * h + b:512 * h + 512:4], T.X[:, c0:c0 + 128], ACT.Exp, scale=A), "ex%d%d" % (h, b))

    def finish(h, quarters):
        wait(V, "e20s")
        if quarters:
            for b in range(4):
                wait(V, "ex%d%d" % (h, b))
                v = T.P[:, 512 * h + b:512 * h + 512:4]
                inc(V.tensor_scalar(v, v, T.e20[:, 0:1], None, ALU.max), "cl%d" % h)
        else:
            for b in range(4):
                wait(V, "ex%d%d" % (h, b))
            inc(V.tensor_scalar(T.P[:, 512 * h:512 * h + 512], T.P[:, 512 * h:512 * h + 512], T.e20[:, 0:1], None, ALU.max),
                "cl%d" % h)
        wait(V, "cl%d" % h)
        inc(V.quantize_mx(T.pc[:, 128 * h:128 * h + 128], T.psc[:, 128 * h:128 * h + 128], T.P[:, 512 * h:512 * h + 512]),
            "qp%d" % h)
        if is_root:
            wait(SY, "cl%d" % h)
            inc(SY.dma_start(T.p[:, 512 * h:512 * h + 512], T.P[:, 512 * h:512 * h + 512]), "outp", 16)
        wait(PE, "qp%d" % h)
        wait(PE, "ldv")
        if core in plan:
            wait(PE, "qone")
        else:
            PE.wait_ge(sem.onearr, 2 * engines(topo.mask(oparent[core], core)))
        inc(PE.matmul_mx(T.ps[:, 3072 + 512 * h:3072 + 512 * h + 130], T.pc[:, 128 * h:128 * h + 128],
                         T.psc[:, 128 * h:128 * h + 128], T.vo[:, 0:130], T.vos[:, 0:130], True, True), "al%d" % h)

    def ship(h):
        wait(S, "al%d" % h)
        inc(scopy(T.msg[:, SL * h:SL * h + 129], T.ps[:, 3072 + 512 * h:3072 + 512 * h + 129]), "ev%d" % h)
        wait(g, "ev%d" % h)
        s0 = SL * (2 * rank + h)
        g.remote_dma(out_ap=T.aland[:, s0:s0 + 129], in_ap=T.msg[:, SL * h:SL * h + 129], remote_sem=sem["ar%d_%d" % (rank, h)],
                     local_sem=sem.sent, pid=pid, routing_id=rid, dma_engine_mask=mk)

    largest(0)
    turn(0)
    spread(V, vcopy, 0, "l")
    spread(S, scopy, 0, "h")
    largest(1)
    sub_exp(0, 0)
    turn(1)
    spread(S, scopy, 1, "l")
    spread(S, scopy, 1, "h")
    if is_root:
        for h in range(2):
            inc(scopy(T.craw[:, 4 * rank + h:4 * rank + h + 1], T.mT[:, 4 * h:4 * h + 1]), "cown")
    else:
        nsent += 2 * engines(mk)
    for h, b in ((0, 1), (0, 2), (0, 3), (1, 0), (1, 1), (1, 2)):
        sub_exp(h, b)
    finish(0, False)
    sub_exp(1, 3)
    if not is_root:
        ship(0)
    finish(1, True)
    if not is_root:
        ship(1)
        nsent += 2 * engines(mk)
        SY.wait_ge(sem.sent, nsent + sentn[0])
        wait(SY, "cl0")
        wait(SY, "cl1")
        inc(SY.dma_start(T.p[:], T.P[:]), "outp", 16)
    for h in range(2):
        for s in ("l", "h"):
            wait(S, "s2_%d%s" % (h, s))
    inc(S.activation(T.crow[0:1, :], T.C[0:1, :], ACT.Identity, scale=A), "cr")
    wait(SY, "cr")
    inc(SY.dma_start(T.c[:], T.crow[0:1, :]), "outc", 16)

    if is_root:
        ncarr = 0
        for r in others:
            ncarr += 2 * engines(topo.mask(T.cores[r], rootc))
        S.wait_ge(sem.carr, ncarr)
        wait(S, "cown")
        for h in range(2):
            inc(S.activation(T.cland[:, h:4 * N:4], T.craw[:, h:4 * N:4], ACT.Identity, scale=A), "ct")
        wait(V, "ct")
        for h in range(2):
            inc(V.tensor_reduce(T.negM[:, h:h + 1], T.cland[:, h:4 * N:4], AX.X, ALU.max, negate=True), "ng")
        wait(S, "ng")
        wait(S, "m_wx")
        for h in range(2):
            inc(S.activation(T.wx[:, 32 * h:32 * h + N], T.cland[:, h:4 * N:4], ACT.Exp, bias=T.negM[:, h:h + 1]), "wxs")
        wait(V, "wxs")
        inc(V.transpose(T.wxt[:], T.wx[:]), "wt")
        wait(SY, "wt")
        for h in range(2):
            for a in range(4):
                c0 = 128 * h + 32 * a
                inc(SY.dma_start(T.w[:, c0:c0 + 32], T.wxt[32 * a:32 * a + N, 32 * h:32 * h + 32]), "outw", 16)
        wait(S, "wxs")
        for h in range(2):
            s0 = SL * (2 * rank + h)
            wait(S, "al%d" % h)
            inc(S.activation(T.tmp[:, s0:s0 + 129], T.ps[:, 3072 + 512 * h:3072 + 512 * h + 129], ACT.Identity,
                             scale=T.wx[:, 32 * h + rank:32 * h + rank + 1]), "tmo%d" % h)

        def weigh(j, h):
            s0 = SL * (2 * j + h)
            S.wait_ge(sem["ar%d_%d" % (j, h)], engines(topo.mask(T.cores[j], rootc)))
            inc(S.activation(T.tmp[:, s0:s0 + 129], T.aland[:, s0:s0 + 129], ACT.Identity,
                             scale=T.wx[:, 32 * h + j:32 * h + j + 1]), "tm%d_%d" % (j, h))

        def add(j, h, first):
            s0 = SL * (2 * j + h)
            a = T.acc[:, SL * h:SL * h + 129]
            wait(V, "tm%d_%d" % (j, h))
            if first:
                wait(V, "tmo%d" % h)
                o0 = SL * (2 * rank + h)
                inc(V.tensor_tensor(a, T.tmp[:, o0:o0 + 129], T.tmp[:, s0:s0 + 129], ALU.add), "ac%d" % h)
            else:
                wait(V, "ac%d" % h)
                inc(V.tensor_tensor(a, a, T.tmp[:, s0:s0 + 129], ALU.add), "ac%d" % h)

        def divide(h):
            wait(V, "ac%d" % h)
            inc(V.reciprocal(T.rdn[:, h:h + 1], T.acc[:, SL * h + 128:SL * h + 129]), "rc%d" % h)
            wait(V, "rc%d" % h)
            inc(V.tensor_scalar(T.Z[:, 128 * h:128 * h + 128], T.acc[:, SL * h:SL * h + 128], T.rdn[:, h:h + 1], None, ALU.mult),
                "z%d" % h)
            wait(V, "z%d" % h)
            inc(V.transpose(T.Zt[:, 128 * h:128 * h + 128], T.Z[:, 128 * h:128 * h + 128]), "zt%d" % h)

        def blocks(h, nv):
            k = 0
            wait(V, "zt%d" % h)
            wait(S, "zt%d" % h)
            for a in range(4):
                for d in range(4):
                    out = T.O[32 * d:32 * d + 32, 128 * h + 32 * a:128 * h + 32 * a + 32]
                    in_ = T.Zt[32 * a:32 * a + 32, 128 * h + 32 * d:128 * h + 32 * d + 32]
                    if k < nv:
                        inc(vcopy(out, in_), "cpv%d" % h)
                    else:
                        inc(scopy(out, in_), "cps%d" % h)
                    k += 1
            if nv:
                wait(SY, "cpv%d" % h)
            wait(SY, "cps%d" % h)
            inc(SY.dma_start(T.o[:, 128 * h:128 * h + 128], T.O[:, 128 * h:128 * h + 128]), "outo", 16)

        for i, j in enumerate(proc[:-1]):
            for h in range(2):
                weigh(j, h)
                add(j, h, i == 0)
        last = proc[-1]
        weigh(last, 0)
        weigh(last, 1)
        add(last, 0, False)
        divide(0)
        blocks(0, 0)
        add(last, 1, False)
        divide(1)
        blocks(1, 10)

    g.wait_ge(sem.sent, nsent + sentn[0])
    for name in sorted(tot):
        if seen.get(name, 0) < tot[name]:
            wait(g, name)
